import numpy as np
import ml_dtypes


def mxq(x, axis, fmt="e4m3"):
    dtype, down = {"e4m3": (ml_dtypes.float8_e4m3fn, 7), "e5m2": (ml_dtypes.float8_e5m2, 14)}[fmt]
    v = np.moveaxis(np.asarray(x, np.float32).astype(ml_dtypes.bfloat16).astype(np.float64), axis, -1)
    blocks = v.reshape(v.shape[:-1] + (-1, 32))
    amax = np.abs(blocks).max(-1, keepdims=True)
    byte = np.maximum(np.where(amax > 0, np.frexp(amax)[1] - 1 + 127, 0) - down, 1)
    scale = np.exp2(byte - 127.0)
    codes = (blocks / scale).astype(np.float32).astype(dtype).astype(np.float64)
    return np.moveaxis((codes * scale).reshape(v.shape), -1, axis)


WIDE = False


def mx_kscale(k):
    if not WIDE:
        return np.ones(k)
    levels = np.array([10, -10, 5, -5, 0])
    if k % 512:
        return np.exp2(np.random.permutation(np.resize(levels, k // 32))).repeat(32)
    a = np.empty((k // 512, 16))
    for p in range(k // 512):
        a[p, :8] = np.random.permutation(np.resize(levels, 8))
        for g in range(8):
            far = levels[np.abs(levels - a[p, g]) >= 10]
            a[p, g + 8] = far[np.random.randint(len(far))]
    return np.exp2(a.ravel()).repeat(32)


BF16 = ml_dtypes.bfloat16


def bf(x):
    return np.asarray(x, np.float32).astype(BF16)


def f64(x):
    return np.asarray(x).astype(np.float64)


E2M1 = np.array([0.0, 0.5, 1.0, 1.5, 2.0, 3.0, 4.0, 6.0, -0.0, -0.5, -1.0, -1.5, -2.0, -3.0, -4.0, -6.0])


def pack_weight(w, fmt):
    k, n = w.shape
    w = f64(bf(w)).reshape(k // 32, 32, n)
    amax = np.abs(w).max(1)
    if fmt == "e4m3":
        byte = np.frexp(amax)[1] - 1 + 127 - 7
    else:
        mant, ex = np.frexp(amax / 6.0)
        byte = np.where(mant > 0.5, ex, ex - 1) + 127
    byte = np.clip(np.where(amax > 0, byte, 1), 1, 254)
    scaled = (w * np.exp2(127.0 - byte)[:, None, :]).reshape(k, n).astype(np.float32)
    by_word = np.ascontiguousarray(scaled.reshape(k // 512, 128, 4, n).transpose(0, 1, 3, 2))
    if fmt == "e4m3":
        words = by_word.astype(ml_dtypes.float8_e4m3fn).view(np.uint8)
    else:
        c = by_word.astype(ml_dtypes.float4_e2m1fn).view(np.uint8) & 0xF
        words = c[..., 0::2] | (c[..., 1::2] << 4)
    return np.ascontiguousarray(words), np.ascontiguousarray(byte.astype(np.uint8).reshape(k // 512, 16, n))


def unpack_weight(words, scales, fmt):
    g, p, n, _ = words.shape
    if fmt == "e4m3":
        vals = np.ascontiguousarray(words).view(ml_dtypes.float8_e4m3fn).astype(np.float64)
    else:
        nib = np.empty((g, p, n, 4), np.uint8)
        nib[..., 0::2] = words & 0xF
        nib[..., 1::2] = words >> 4
        vals = E2M1[nib]
    vals = vals * np.repeat(np.exp2(scales.astype(np.float64) - 127.0), 8, axis=1)[..., None]
    return vals.transpose(0, 1, 3, 2).reshape(g * 512, n)
def pack4(w):
    words, scales = pack_weight(w, "e2m1")
    return words.reshape(words.shape[0], 128, -1), scales


def unpack4(words, scales):
    return unpack_weight(words.reshape(words.shape[0], 128, -1, 2), scales, "e2m1")


M, D, R, N = 768, 1024, 512, 2048


def setup_inputs():
    s = mx_kscale(D)
    u = mx_kscale(R)
    t = mx_kscale(N)
    x = bf(np.random.standard_normal((M, D)) * s)
    qv_words, qv_scales = pack4(0.6 * np.random.standard_normal((D, N)) / np.sqrt(D) / s[:, None])
    y = bf(np.random.standard_normal((M, R)) * u)
    b = bf(0.6 * np.random.standard_normal((R, N)) / np.sqrt(R) / u[:, None])
    r = bf((1 + 0.1 * np.random.standard_normal(N)) * t)
    v_words, v_scales = pack4(np.random.standard_normal((N, D)) / np.sqrt(N) / t[:, None])
    return {"x": x, "qv_words": qv_words, "qv_scales": qv_scales, "y": y, "b": b,
            "r": r, "v_words": v_words, "v_scales": v_scales}


def reference(x, qv_words, qv_scales, y, b, r, v_words, v_scales):
    qv = unpack4(qv_words, qv_scales)
    v = unpack4(v_words, v_scales)
    grad = (mxq(f64(x), 1, "e4m3") @ qv) + (mxq(f64(y), 1, "e4m3") @ mxq(f64(b), 0, "e4m3"))
    e = np.exp(-grad)
    z = e.mean(axis=1)
    w = e * f64(r)
    step = mxq(w, 1, "e4m3") @ v
    return step, z

@@ -1,0 +1,316 @@
+from contextlib import ExitStack
+
+import concourse.mybir as mybir
+from concourse.masks import make_identity
+
+M, D, R, N = 768, 1024, 512, 2048
+FLOPS = 2 * M * N * (D + R) + 2 * M * N * D
+
+F32 = mybir.dt.float32
+BF16 = mybir.dt.bfloat16
+I32 = mybir.dt.int32
+U32 = mybir.dt.uint32
+U8 = mybir.dt.uint8
+FP8X4 = mybir.dt.float8_e4m3fn_x4
+FP4X4 = mybir.dt.float4_e2m1fn_x4
+ACT = mybir.ActivationFunctionType
+ALU = mybir.AluOpType
+
+P = 128
+W = 512
+TILES = M // P
+CHUNKS = N // W
+EARLY = 3
+B0_VECTOR_COLS = 320
+
+
+def tile_soft_frank_wolfe_vertex_s3_kernel(tc, x, qv_words, qv_scales, y, b, r, v_words, v_scales, out_0, out_1):
+    nc = tc.nc
+    order = [(i, j) for j in range(CHUNKS) for i in range(EARLY)]
+    order = order + [(i, j) for i in range(EARLY, TILES) for j in range(CHUNKS)]
+
+    with ExitStack() as ctx:
+        keep = ctx.enter_context(tc.tile_pool(name="keep", bufs=1))
+        ring = ctx.enter_context(tc.tile_pool(name="ring", bufs=1))
+        psum = ctx.enter_context(tc.psum_pool(name="psum", bufs=8))
+        ctx.enter_context(tc.manual_schedule())
+
+        def kept(name, shape, dtype):
+            return keep.tile(shape, dtype, name=name, tag=name, align_bytes=64)
+
+        def ringed(tag, bufs, name, shape, dtype):
+            return ring.tile(shape, dtype, name=name, tag=tag, bufs=bufs, align_bytes=64)
+
+        def bank(name, shape):
+            return psum.tile(shape, F32, name=name, tag="bank")
+
+        qs_first = kept("qs_first", [P, 2, W], U8)
+        qs_rest = kept("qs_rest", [P, 2, N - W], U8)
+        vs = kept("vs", [P, CHUNKS, D], U8)
+        r_row = kept("r_row", [P, N], BF16)
+        z_cols = kept("z_cols", [P, P], F32)
+        z_parts = kept("z_parts", [P, TILES * CHUNKS], F32)
+        ident = kept("ident", [P, P], F32)
+        ones = kept("ones", [P, P], BF16)
+
+        nc.vector.memset(qs_first[:].rearrange("p g n -> p (g n)").bitcast(I32), 0)
+        nc.vector.memset(z_cols[:], 0.0)
+        nc.vector.memset(r_row[:].bitcast(I32), 0)
+        nc.vector.memset(qs_rest[:].rearrange("p g n -> p (g n)").bitcast(I32), 0)
+        nc.vector.memset(vs[:].rearrange("p g n -> p (g n)").bitcast(I32), 0)
+        make_identity(nc, ident[:])
+        nc.scalar.activation(out=ones[:], in_=z_cols[:], func=ACT.Exp)
+
+        rows = {}
+        b_raw, qv, v = {}, {}, {}
+
+        def load_x(i):
+            rows["x%d" % i] = kept("x%d" % i, [P, D], BF16)
+            nc.sync.dma_start(out=rows["x%d" % i][:], in_=x[i * P : (i + 1) * P, :])
+
+        def load_x_pair(i):
+            pair = kept("x_pair%d" % i, [P, 2 * D], BF16)
+            rows["x%d" % i] = pair[:, 0:D]
+            rows["x%d" % (i + 1)] = pair[:, D : 2 * D]
+            nc.sync.dma_start(
+                out=pair[:].rearrange("p (a k) -> p a k", a=2),
+                in_=x[i * P : (i + 2) * P, :].rearrange("(a p) k -> p a k", a=2),
+            )
+
+        def load_y(a):
+            rows["y%d" % a] = kept("y%d" % a, [P, 2 * R], BF16)
+            nc.sync.dma_start(
+                out=rows["y%d" % a][:].rearrange("p (a k) -> p a k", a=2),
+                in_=y[2 * a * P : 2 * (a + 1) * P, :].rearrange("(a p) k -> p a k", a=2),
+            )
+
+        def load_b(j):
+            b_raw[j] = kept("b_raw%d" % j, [P, 4, W], BF16)
+            nc.sync.dma_start(out=b_raw[j][:], in_=b[:, j * W : (j + 1) * W].rearrange("(p t) n -> p t n", t=4))
+
+        def load_qv(j):
+            qv[j] = kept("qv%d" % j, [P, 2, 2 * W], U8)
+            nc.sync.dma_start(
+                out=qv[j][:].bitcast(I32),
+                in_=qv_words.bitcast(I32)[:, :, j * W // 2 : (j + 1) * W // 2].rearrange("g p n -> p g n"),
+            )
+
+        def load_v(h):
+            v[h] = kept("v%d" % h, [P, CHUNKS, 2 * W], U8)
+            nc.sync.dma_start(
+                out=v[h][:].bitcast(I32),
+                in_=v_words.bitcast(I32)[:, :, h * W // 2 : (h + 1) * W // 2].rearrange("g p n -> p g n"),
+            )
+
+        def load_scales(plane, scales, c0, c1):
+            by_row = scales.bitcast(I32)[:, :, c0 // 4 : c1 // 4].rearrange("g (q s) n -> s q g n", s=4)
+            for s in range(4):
+                nc.sync.dma_start(out=plane[s:P:32].bitcast(I32), in_=by_row[s])
+
+        load_x(0)
+        load_y(0)
+        load_b(0)
+        load_qv(0)
+        load_scales(qs_first, qv_scales, 0, W)
+        load_x_pair(1)
+        load_y(1)
+        load_b(1)
+        nc.sync.dma_start(out=r_row[0:1, :], in_=r.rearrange("(o n) -> o n", o=1))
+        load_qv(1)
+        load_scales(qs_rest, qv_scales, W, N)
+        load_b(2)
+        load_qv(2)
+        load_b(3)
+        load_qv(3)
+        load_x(3)
+        load_y(2)
+        load_x(4)
+        load_x(5)
+        load_scales(vs, v_scales, 0, D)
+        load_v(0)
+        load_v(1)
+
+        engines = {"S": nc.scalar.copy, "V": nc.vector.tensor_copy}
+        in_order, grouped, codes, scales = {}, {}, {}, {}
+        b_grouped, r_sorted, g_bank, e = {}, {}, {}, {}
+
+        def presort(u):
+            in_order[u] = ringed("sorted", 4, "sorted_" + u, [P, 4, P], F32)
+            nc.vector.tensor_copy(
+                out=in_order[u][:].rearrange("p (g u) w -> p g u w", u=2),
+                in_=rows[u][:, :].bitcast(F32).rearrange("p (g w u) -> p g u w", g=2, u=2),
+            )
+
+        def turn(units, engs):
+            banks = []
+            for u in units:
+                t = bank("t_" + u, [P, 4, P])
+                banks.append(t)
+                for q in range(4):
+                    if u in in_order:
+                        src = in_order[u][:, q, :]
+                    else:
+                        src = rows[u][:, :].bitcast(F32)[:, 256 * (q // 2) + q % 2 : 256 * (q // 2 + 1) : 2]
+                    nc.tensor.transpose(t[:, q, :], src, ident[:])
+            for u, t, eng in zip(units, banks, engs):
+                grouped[u] = ringed("grouped", 8, "grouped_" + u, [P, 2 * W], BF16)
+                engines[eng](
+                    out=grouped[u][:].bitcast(F32).rearrange("p (a m u) -> p a m u", a=2, u=2),
+                    in_=t[:].rearrange("p (a u) m -> p a m u", u=2),
+                )
+
+        def quantise(key, src, width):
+            codes[key] = kept("codes_" + key, [P, width], U32)
+            scales[key] = kept("scales_" + key, [P, width], U8)
+            nc.vector.quantize_mx(out=codes[key][:].bitcast(FP8X4), scales=scales[key][:], in_=src)
+
+        def quant(units):
+            for u in units:
+                quantise(u, grouped[u][:], 2 * P)
+
+        def interleave(j, eng, c0, c1):
+            if j not in b_grouped:
+                b_grouped[j] = ringed("b_grouped", 2, "b_grouped%d" % j, [P, W, 4], BF16)
+            engines[eng](
+                out=b_grouped[j][:, c0:c1, :].rearrange("p (c i) t -> p c t i", i=4),
+                in_=b_raw[j][:, :, c0:c1].rearrange("p t (c i) -> p c t i", i=4),
+            )
+
+        def quant_b(j):
+            quantise("b%d" % j, b_grouped[j][:].rearrange("p n t -> p (n t)"), W)
+
+        r_bank = {}
+
+        def spread_r(j):
+            r_bank[j] = bank("r_bank%d" % j, [P, W])
+            nc.tensor.matmul(r_bank[j][:], lhsT=ones[:], rhs=r_row[:, j * W : (j + 1) * W], start=True, stop=True)
+
+        def fetch_r(j):
+            r_sorted[j] = kept("r_sorted%d" % j, [P, W], BF16)
+            nc.scalar.copy(
+                out=r_sorted[j][:].rearrange("m (u p e) -> m u p e", u=2, e=2),
+                in_=r_bank[j][:].rearrange("m (p u e) -> m u p e", u=2, e=2),
+            )
+
+        def mx(acc, key, half, rhs, rhs_scale, start, stop):
+            cols = slice(half * P, (half + 1) * P)
+            nc.tensor.matmul_mx(
+                out=acc[:], lhsT=codes[key][:, cols].bitcast(FP8X4), lhsT_scale=scales[key][:, cols],
+                rhs=rhs, rhs_scale=rhs_scale, start=start, stop=stop,
+            )
+
+        def grad_x(s):
+            i, j = order[s]
+            g_bank[s] = bank("g%d" % s, [P, W])
+            for g in range(2):
+                plane = qs_first[:, g, :] if j == 0 else qs_rest[:, g, (j - 1) * W : j * W]
+                mx(g_bank[s], "x%d" % i, g, qv[j][:, g, :].bitcast(FP4X4), plane, g == 0, False)
+
+        def grad_y(s):
+            i, j = order[s]
+            key = "b%d" % j
+            mx(g_bank[s], "y%d" % (i // 2), i % 2, codes[key][:].bitcast(FP8X4), scales[key][:], False, True)
+            e[s] = ringed("e", 12, "e%d" % s, [P, W], F32)
+            col = i * CHUNKS + j
+            nc.scalar.activation(
+                out=e[s][:].rearrange("m (u p e) -> m u p e", u=2, e=2),
+                in_=g_bank[s][:].rearrange("m (p u e) -> m u p e", u=2, e=2),
+                func=ACT.Exp, scale=-1.0, accum_out=z_parts[:, col : col + 1],
+            )
+
+        h_rows = {}
+
+        def weigh(s):
+            u = "h%d" % (s // 2)
+            if s % 2 == 0:
+                h_rows[u] = ringed("h_rows", 8, "rows_" + u, [P, 2 * W], BF16)
+                in_order[u] = h_rows[u][:, :].bitcast(F32).rearrange("p (q w) -> p q w", q=4)
+            half = s % 2
+            nc.vector.tensor_tensor(
+                out=h_rows[u][:, half * W : (half + 1) * W], in0=e[s][:], in1=r_sorted[order[s][1]][:], op=ALU.mult
+            )
+
+        def step_cols(i, c0, width, eng):
+            h = c0 // W
+            acc = bank("o%d_%d" % (i, c0), [P, width])
+            for j in range(CHUNKS):
+                s = order.index((i, j))
+                words = v[h][:, j, 2 * (c0 - h * W) : 2 * (c0 - h * W + width)]
+                mx(acc, "h%d" % (s // 2), s % 2, words.bitcast(FP4X4), vs[:, j, c0 : c0 + width], j == 0, j == CHUNKS - 1)
+            res = ringed("res", 6, "res%d_%d" % (i, c0), [P, width], F32)
+            engines[eng](out=res[:], in_=acc[:])
+            nc.sync.dma_start(out=out_0[i * P : (i + 1) * P, c0 : c0 + width], in_=res[:])
+
+        turn(["x0", "y0"], "SV")
+        quant(["x0"])
+        interleave(0, "V", 0, B0_VECTOR_COLS)
+        interleave(0, "S", B0_VECTOR_COLS, W)
+        quant(["y0"])
+        quant_b(0)
+        grad_x(0)
+        turn(["x1"], "S")
+        quant(["x1"])
+        grad_y(0)
+        turn(["x2", "y1"], "SS")
+        spread_r(0)
+        spread_r(1)
+        interleave(1, "V", 0, W)
+        quant(["x2", "y1"])
+        quant_b(1)
+        fetch_r(0)
+        fetch_r(1)
+
+        turns = {
+            10: (["x3", "y2", "x4", "x5"], "SSSS"),
+            15: (["h0", "h1", "h2", "h3"], "SSSS"),
+            19: (["h4", "h5", "h6", "h7"], "SVSS"),
+        }
+        steps_at = {21: 0, 22: 1}
+        interleave_at = {1: 2, 3: 3}
+        quant_b_at = {2: 2, 4: 3}
+        weighed = 0
+        for s in range(1, len(order)):
+            if s == 2:
+                for j in (2, 3):
+                    spread_r(j)
+                    fetch_r(j)
+            if s in turns:
+                turn(*turns[s])
+            if s in steps_at:
+                step_cols(steps_at[s], 0, W, "V")
+                step_cols(steps_at[s], W, W, "S")
+            if s in interleave_at:
+                interleave(interleave_at[s], "V", 0, W)
+            if s == 7:
+                for u in turns[10][0]:
+                    presort(u)
+            if s in quant_b_at:
+                quant_b(quant_b_at[s])
+            grad_x(s)
+            grad_y(s)
+            if s in turns:
+                quant(turns[s][0])
+            if s >= 8:
+                upto = min(weighed + 2, s)
+                for t in range(weighed, upto):
+                    weigh(t)
+                weighed = upto
+        weigh(len(order) - 1)
+        nc.vector.tensor_reduce(
+            out=z_cols[:, 0:TILES], in_=z_parts[:].rearrange("p (i j) -> p i j", j=CHUNKS), axis=mybir.AxisListType.X, op=ALU.add
+        )
+        step_cols(2, 0, W, "S")
+        step_cols(2, W, W, "S")
+        turn(["h8", "h9", "h10", "h11"], "VSVS")
+        z_bank = bank("z_bank", [P, P])
+        nc.tensor.transpose(z_bank[:], z_cols[:], ident[:])
+        quant(["h8", "h9", "h10", "h11"])
+        z_rows = kept("z_rows", [32, P], F32)
+        nc.scalar.activation(out=z_rows[:], in_=z_bank[0:32, :], func=ACT.Copy, scale=1.0 / N)
+        nc.sync.dma_start(out=out_1.rearrange("(i p) -> i p", p=P), in_=z_rows[0:TILES, :])
+        for i in (3, 4):
+            step_cols(i, 0, W, "V")
+            step_cols(i, W, W, "S")
+        step_cols(5, 0, W, "V")
+        for c in range(4):
+            step_cols(5, W + c * P, P, "SV"[c % 2])

@@ -22,6 +22,7 @@ TILES = M // P
 CHUNKS = N // W
 EARLY = 3
 B0_VECTOR_COLS = 320
+WARM_UPS = 4
 
 
 def tile_soft_frank_wolfe_vertex_s3_kernel(tc, x, qv_words, qv_scales, y, b, r, v_words, v_scales, out_0, out_1):
@@ -53,13 +54,17 @@ def tile_soft_frank_wolfe_vertex_s3_kernel(tc, x, qv_words, qv_scales, y, b, r, 
         ident = kept("ident", [P, P], F32)
         ones = kept("ones", [P, P], BF16)
 
-        nc.vector.memset(qs_first[:].rearrange("p g n -> p (g n)").bitcast(I32), 0)
-        nc.vector.memset(z_cols[:], 0.0)
+        nc.gpsimd.memset(z_cols[:], 0.0)
+        nc.gpsimd.memset(qs_first[:].rearrange("p g n -> p (g n)").bitcast(I32), 0)
         nc.vector.memset(r_row[:].bitcast(I32), 0)
         nc.vector.memset(qs_rest[:].rearrange("p g n -> p (g n)").bitcast(I32), 0)
         nc.vector.memset(vs[:].rearrange("p g n -> p (g n)").bitcast(I32), 0)
         make_identity(nc, ident[:])
         nc.scalar.activation(out=ones[:], in_=z_cols[:], func=ACT.Exp)
+
+        warm = bank("warm", [P, P])
+        for w in range(WARM_UPS):
+            nc.tensor.matmul(warm[:], lhsT=z_cols[:], rhs=z_cols[:], start=True, stop=True)
 
         rows = {}
         b_raw, qv, v = {}, {}, {}
@@ -67,15 +72,6 @@ def tile_soft_frank_wolfe_vertex_s3_kernel(tc, x, qv_words, qv_scales, y, b, r, 
         def load_x(i):
             rows["x%d" % i] = kept("x%d" % i, [P, D], BF16)
             nc.sync.dma_start(out=rows["x%d" % i][:], in_=x[i * P : (i + 1) * P, :])
-
-        def load_x_pair(i):
-            pair = kept("x_pair%d" % i, [P, 2 * D], BF16)
-            rows["x%d" % i] = pair[:, 0:D]
-            rows["x%d" % (i + 1)] = pair[:, D : 2 * D]
-            nc.sync.dma_start(
-                out=pair[:].rearrange("p (a k) -> p a k", a=2),
-                in_=x[i * P : (i + 2) * P, :].rearrange("(a p) k -> p a k", a=2),
-            )
 
         def load_y(a):
             rows["y%d" % a] = kept("y%d" % a, [P, 2 * R], BF16)
@@ -109,13 +105,14 @@ def tile_soft_frank_wolfe_vertex_s3_kernel(tc, x, qv_words, qv_scales, y, b, r, 
 
         load_x(0)
         load_y(0)
+        load_scales(qs_first, qv_scales, 0, W)
+        nc.sync.dma_start(out=r_row[0:1, :], in_=r.rearrange("(o n) -> o n", o=1))
         load_b(0)
         load_qv(0)
-        load_scales(qs_first, qv_scales, 0, W)
-        load_x_pair(1)
+        load_x(1)
+        load_x(2)
         load_y(1)
         load_b(1)
-        nc.sync.dma_start(out=r_row[0:1, :], in_=r.rearrange("(o n) -> o n", o=1))
         load_qv(1)
         load_scales(qs_rest, qv_scales, W, N)
         load_b(2)
@@ -185,9 +182,9 @@ def tile_soft_frank_wolfe_vertex_s3_kernel(tc, x, qv_words, qv_scales, y, b, r, 
             r_bank[j] = bank("r_bank%d" % j, [P, W])
             nc.tensor.matmul(r_bank[j][:], lhsT=ones[:], rhs=r_row[:, j * W : (j + 1) * W], start=True, stop=True)
 
-        def fetch_r(j):
+        def fetch_r(j, eng):
             r_sorted[j] = kept("r_sorted%d" % j, [P, W], BF16)
-            nc.scalar.copy(
+            engines[eng](
                 out=r_sorted[j][:].rearrange("m (u p e) -> m u p e", u=2, e=2),
                 in_=r_bank[j][:].rearrange("m (p u e) -> m u p e", u=2, e=2),
             )
@@ -210,7 +207,7 @@ def tile_soft_frank_wolfe_vertex_s3_kernel(tc, x, qv_words, qv_scales, y, b, r, 
             i, j = order[s]
             key = "b%d" % j
             mx(g_bank[s], "y%d" % (i // 2), i % 2, codes[key][:].bitcast(FP8X4), scales[key][:], False, True)
-            e[s] = ringed("e", 12, "e%d" % s, [P, W], F32)
+            e[s] = ringed("e", 13, "e%d" % s, [P, W], F32)
             col = i * CHUNKS + j
             nc.scalar.activation(
                 out=e[s][:].rearrange("m (u p e) -> m u p e", u=2, e=2),
@@ -223,7 +220,7 @@ def tile_soft_frank_wolfe_vertex_s3_kernel(tc, x, qv_words, qv_scales, y, b, r, 
         def weigh(s):
             u = "h%d" % (s // 2)
             if s % 2 == 0:
-                h_rows[u] = ringed("h_rows", 8, "rows_" + u, [P, 2 * W], BF16)
+                h_rows[u] = ringed("h_rows", 9, "rows_" + u, [P, 2 * W], BF16)
                 in_order[u] = h_rows[u][:, :].bitcast(F32).rearrange("p (q w) -> p q w", q=4)
             half = s % 2
             nc.vector.tensor_tensor(
@@ -242,38 +239,37 @@ def tile_soft_frank_wolfe_vertex_s3_kernel(tc, x, qv_words, qv_scales, y, b, r, 
             nc.sync.dma_start(out=out_0[i * P : (i + 1) * P, c0 : c0 + width], in_=res[:])
 
         turn(["x0", "y0"], "SV")
+        for j in range(CHUNKS):
+            spread_r(j)
         quant(["x0"])
+        fetch_r(0, "S")
         interleave(0, "V", 0, B0_VECTOR_COLS)
         interleave(0, "S", B0_VECTOR_COLS, W)
         quant(["y0"])
+        fetch_r(1, "V")
         quant_b(0)
         grad_x(0)
-        turn(["x1"], "S")
+        fetch_r(2, "V")
+        fetch_r(3, "S")
+        turn(["x1", "x2", "y1"], "SSS")
         quant(["x1"])
         grad_y(0)
-        turn(["x2", "y1"], "SS")
-        spread_r(0)
-        spread_r(1)
-        interleave(1, "V", 0, W)
+        interleave(1, "V", 0, W // 2)
         quant(["x2", "y1"])
+        interleave(1, "V", W // 2, W)
         quant_b(1)
-        fetch_r(0)
-        fetch_r(1)
 
         turns = {
             10: (["x3", "y2", "x4", "x5"], "SSSS"),
-            15: (["h0", "h1", "h2", "h3"], "SSSS"),
-            19: (["h4", "h5", "h6", "h7"], "SVSS"),
+            16: (["h0", "h1", "h2", "h3"], "SSSS"),
+            20: (["h4", "h5", "h6", "h7"], "SVSS"),
         }
-        steps_at = {21: 0, 22: 1}
+        quant_at = {10: 10, 17: 16, 21: 20}
+        steps_at = {22: 0, 23: 1}
         interleave_at = {1: 2, 3: 3}
         quant_b_at = {2: 2, 4: 3}
         weighed = 0
         for s in range(1, len(order)):
-            if s == 2:
-                for j in (2, 3):
-                    spread_r(j)
-                    fetch_r(j)
             if s in turns:
                 turn(*turns[s])
             if s in steps_at:
@@ -288,10 +284,10 @@ def tile_soft_frank_wolfe_vertex_s3_kernel(tc, x, qv_words, qv_scales, y, b, r, 
                 quant_b(quant_b_at[s])
             grad_x(s)
             grad_y(s)
-            if s in turns:
-                quant(turns[s][0])
+            if s in quant_at:
+                quant(turns[quant_at[s]][0])
             if s >= 8:
-                upto = min(weighed + 2, s)
+                upto = min(weighed + (1 if s < 10 else 2), s)
                 for t in range(weighed, upto):
                     weigh(t)
                 weighed = upto

@@ -20,9 +20,10 @@ P = 128
 W = 512
 TILES = M // P
 CHUNKS = N // W
-EARLY = 3
+EARLY = 4
 B0_VECTOR_COLS = 320
 WARM_UPS = 4
+B1_VECTOR_COLS = 352
 
 
 def tile_soft_frank_wolfe_vertex_s3_kernel(tc, x, qv_words, qv_scales, y, b, r, v_words, v_scales, out_0, out_1):
@@ -67,7 +68,8 @@ def tile_soft_frank_wolfe_vertex_s3_kernel(tc, x, qv_words, qv_scales, y, b, r, 
             nc.tensor.matmul(warm[:], lhsT=z_cols[:], rhs=z_cols[:], start=True, stop=True)
 
         rows = {}
-        b_raw, qv, v = {}, {}, {}
+        b_raw, qv = {}, {}
+        v = kept("v", [P, CHUNKS, 2 * D], U8)
 
         def load_x(i):
             rows["x%d" % i] = kept("x%d" % i, [P, D], BF16)
@@ -84,18 +86,13 @@ def tile_soft_frank_wolfe_vertex_s3_kernel(tc, x, qv_words, qv_scales, y, b, r, 
             b_raw[j] = kept("b_raw%d" % j, [P, 4, W], BF16)
             nc.sync.dma_start(out=b_raw[j][:], in_=b[:, j * W : (j + 1) * W].rearrange("(p t) n -> p t n", t=4))
 
-        def load_qv(j):
-            qv[j] = kept("qv%d" % j, [P, 2, 2 * W], U8)
+        def load_qv(j, count):
+            both = kept("qv%d" % j, [P, 2, count * 2 * W], U8)
+            for c in range(count):
+                qv[j + c] = both[:, :, c * 2 * W : (c + 1) * 2 * W]
             nc.sync.dma_start(
-                out=qv[j][:].bitcast(I32),
-                in_=qv_words.bitcast(I32)[:, :, j * W // 2 : (j + 1) * W // 2].rearrange("g p n -> p g n"),
-            )
-
-        def load_v(h):
-            v[h] = kept("v%d" % h, [P, CHUNKS, 2 * W], U8)
-            nc.sync.dma_start(
-                out=v[h][:].bitcast(I32),
-                in_=v_words.bitcast(I32)[:, :, h * W // 2 : (h + 1) * W // 2].rearrange("g p n -> p g n"),
+                out=both[:].bitcast(I32),
+                in_=qv_words.bitcast(I32)[:, :, j * W // 2 : (j + count) * W // 2].rearrange("g p n -> p g n"),
             )
 
         def load_scales(plane, scales, c0, c1):
@@ -108,24 +105,22 @@ def tile_soft_frank_wolfe_vertex_s3_kernel(tc, x, qv_words, qv_scales, y, b, r, 
         load_scales(qs_first, qv_scales, 0, W)
         nc.sync.dma_start(out=r_row[0:1, :], in_=r.rearrange("(o n) -> o n", o=1))
         load_b(0)
-        load_qv(0)
+        load_qv(0, 1)
         load_x(1)
         load_x(2)
         load_y(1)
+        load_x(3)
         load_b(1)
-        load_qv(1)
+        load_qv(1, 1)
         load_scales(qs_rest, qv_scales, W, N)
         load_b(2)
-        load_qv(2)
+        load_qv(2, 2)
         load_b(3)
-        load_qv(3)
-        load_x(3)
         load_y(2)
         load_x(4)
         load_x(5)
         load_scales(vs, v_scales, 0, D)
-        load_v(0)
-        load_v(1)
+        nc.sync.dma_start(out=v[:].bitcast(I32), in_=v_words.bitcast(I32).rearrange("g p n -> p g n"))
 
         engines = {"S": nc.scalar.copy, "V": nc.vector.tensor_copy}
         in_order, grouped, codes, scales = {}, {}, {}, {}
@@ -134,8 +129,8 @@ def tile_soft_frank_wolfe_vertex_s3_kernel(tc, x, qv_words, qv_scales, y, b, r, 
         def presort(u):
             in_order[u] = ringed("sorted", 4, "sorted_" + u, [P, 4, P], F32)
             nc.vector.tensor_copy(
-                out=in_order[u][:].rearrange("p (g u) w -> p g u w", u=2),
-                in_=rows[u][:, :].bitcast(F32).rearrange("p (g w u) -> p g u w", g=2, u=2),
+                out=in_order[u][:].rearrange("p (g u) (c i) -> p g c u i", u=2, i=4),
+                in_=rows[u][:, :].bitcast(F32).rearrange("p (g c i u) -> p g c u i", g=2, i=4, u=2),
             )
 
         def turn(units, engs):
@@ -207,7 +202,7 @@ def tile_soft_frank_wolfe_vertex_s3_kernel(tc, x, qv_words, qv_scales, y, b, r, 
             i, j = order[s]
             key = "b%d" % j
             mx(g_bank[s], "y%d" % (i // 2), i % 2, codes[key][:].bitcast(FP8X4), scales[key][:], False, True)
-            e[s] = ringed("e", 13, "e%d" % s, [P, W], F32)
+            e[s] = ringed("e", 14, "e%d" % s, [P, W], F32)
             col = i * CHUNKS + j
             nc.scalar.activation(
                 out=e[s][:].rearrange("m (u p e) -> m u p e", u=2, e=2),
@@ -228,11 +223,10 @@ def tile_soft_frank_wolfe_vertex_s3_kernel(tc, x, qv_words, qv_scales, y, b, r, 
             )
 
         def step_cols(i, c0, width, eng):
-            h = c0 // W
             acc = bank("o%d_%d" % (i, c0), [P, width])
             for j in range(CHUNKS):
                 s = order.index((i, j))
-                words = v[h][:, j, 2 * (c0 - h * W) : 2 * (c0 - h * W + width)]
+                words = v[:, j, 2 * c0 : 2 * (c0 + width)]
                 mx(acc, "h%d" % (s // 2), s % 2, words.bitcast(FP4X4), vs[:, j, c0 : c0 + width], j == 0, j == CHUNKS - 1)
             res = ringed("res", 6, "res%d_%d" % (i, c0), [P, width], F32)
             engines[eng](out=res[:], in_=acc[:])
@@ -251,60 +245,63 @@ def tile_soft_frank_wolfe_vertex_s3_kernel(tc, x, qv_words, qv_scales, y, b, r, 
         grad_x(0)
         fetch_r(2, "V")
         fetch_r(3, "S")
-        turn(["x1", "x2", "y1"], "SSS")
+        turn(["x1", "x2", "y1", "x3"], "SSSS")
         quant(["x1"])
         grad_y(0)
-        interleave(1, "V", 0, W // 2)
-        quant(["x2", "y1"])
-        interleave(1, "V", W // 2, W)
+        quant(["x2", "y1", "x3"])
+        interleave(1, "V", 0, B1_VECTOR_COLS)
+        interleave(1, "S", B1_VECTOR_COLS, W)
         quant_b(1)
 
-        turns = {
-            10: (["x3", "y2", "x4", "x5"], "SSSS"),
-            16: (["h0", "h1", "h2", "h3"], "SSSS"),
-            20: (["h4", "h5", "h6", "h7"], "SVSS"),
-        }
-        quant_at = {10: 10, 17: 16, 21: 20}
-        steps_at = {22: 0, 23: 1}
-        interleave_at = {1: 2, 3: 3}
-        quant_b_at = {2: 2, 4: 3}
-        weighed = 0
+        late_rows = ["y2", "x4", "x5"]
+        first_h = ["h0", "h2", "h4", "h6"]
+        second_h = ["h1", "h3", "h5", "h7"]
+        third_h = ["h8", "h9", "h10", "h11"]
+        to_weigh = [s for s in range(16) if s % 4 < 2] + [s for s in range(16) if s % 4 >= 2] + list(range(16, 24))
         for s in range(1, len(order)):
-            if s in turns:
-                turn(*turns[s])
-            if s in steps_at:
-                step_cols(steps_at[s], 0, W, "V")
-                step_cols(steps_at[s], W, W, "S")
-            if s in interleave_at:
-                interleave(interleave_at[s], "V", 0, W)
-            if s == 7:
-                for u in turns[10][0]:
+            if s == 13:
+                turn(late_rows, "SSS")
+            if s == 19:
+                turn(first_h, "SSSS")
+            if s in (4, 7):
+                interleave(2 + (s - 4) // 3, "V", 0, W)
+            if s in (5, 8):
+                quant_b(2 + (s - 5) // 3)
+            if s == 10:
+                for u in late_rows:
                     presort(u)
-            if s in quant_b_at:
-                quant_b(quant_b_at[s])
-            grad_x(s)
+            if s in (4, 8):
+                grad_x(s)
+                grad_x(s + 1)
+            elif s not in (5, 9):
+                grad_x(s)
             grad_y(s)
-            if s in quant_at:
-                quant(turns[quant_at[s]][0])
-            if s >= 8:
-                upto = min(weighed + (1 if s < 10 else 2), s)
-                for t in range(weighed, upto):
+            if s == 13:
+                quant(late_rows)
+            if s == 20:
+                quant(first_h)
+            if s >= 11 and s != 13:
+                for t in [t for t in to_weigh if t < s][:2]:
                     weigh(t)
-                weighed = upto
+                    to_weigh.remove(t)
         weigh(len(order) - 1)
         nc.vector.tensor_reduce(
             out=z_cols[:, 0:TILES], in_=z_parts[:].rearrange("p (i j) -> p i j", j=CHUNKS), axis=mybir.AxisListType.X, op=ALU.add
         )
-        step_cols(2, 0, W, "S")
-        step_cols(2, W, W, "S")
-        turn(["h8", "h9", "h10", "h11"], "VSVS")
+        turn(second_h, "SSSS")
+        step_cols(0, 0, W, "S")
+        quant(second_h)
+        step_cols(0, W, W, "S")
+        step_cols(1, 0, W, "V")
+        step_cols(1, W, W, "S")
+        turn(third_h, "VSVS")
         z_bank = bank("z_bank", [P, P])
         nc.tensor.transpose(z_bank[:], z_cols[:], ident[:])
-        quant(["h8", "h9", "h10", "h11"])
+        quant(third_h)
         z_rows = kept("z_rows", [32, P], F32)
         nc.scalar.activation(out=z_rows[:], in_=z_bank[0:32, :], func=ACT.Copy, scale=1.0 / N)
         nc.sync.dma_start(out=out_1.rearrange("(i p) -> i p", p=P), in_=z_rows[0:TILES, :])
-        for i in (3, 4):
+        for i in (2, 3, 4):
             step_cols(i, 0, W, "V")
             step_cols(i, W, W, "S")
         step_cols(5, 0, W, "V")

from contextlib import ExitStack

import concourse.mybir as mybir
from concourse.masks import make_identity

M, D, R, N = 768, 1024, 512, 2048
FLOPS = 2 * M * N * (D + R) + 2 * M * N * D

F32 = mybir.dt.float32
BF16 = mybir.dt.bfloat16
I32 = mybir.dt.int32
U32 = mybir.dt.uint32
U8 = mybir.dt.uint8
FP8X4 = mybir.dt.float8_e4m3fn_x4
FP4X4 = mybir.dt.float4_e2m1fn_x4
ACT = mybir.ActivationFunctionType
ALU = mybir.AluOpType

P = 128
W = 512
TILES = M // P
CHUNKS = N // W
EARLY = 4
B0_VECTOR_COLS = 320
WARM_UPS = 4
B1_VECTOR_COLS = 352


def tile_soft_frank_wolfe_vertex_s3_kernel(tc, x, qv_words, qv_scales, y, b, r, v_words, v_scales, out_0, out_1):
    nc = tc.nc
    order = [(i, j) for j in range(CHUNKS) for i in range(EARLY)]
    order = order + [(i, j) for i in range(EARLY, TILES) for j in range(CHUNKS)]

    with ExitStack() as ctx:
        keep = ctx.enter_context(tc.tile_pool(name="keep", bufs=1))
        ring = ctx.enter_context(tc.tile_pool(name="ring", bufs=1))
        psum = ctx.enter_context(tc.psum_pool(name="psum", bufs=8))
        ctx.enter_context(tc.manual_schedule())

        def kept(name, shape, dtype):
            return keep.tile(shape, dtype, name=name, tag=name, align_bytes=64)

        def ringed(tag, bufs, name, shape, dtype):
            return ring.tile(shape, dtype, name=name, tag=tag, bufs=bufs, align_bytes=64)

        def bank(name, shape):
            return psum.tile(shape, F32, name=name, tag="bank")

        qs_first = kept("qs_first", [P, 2, W], U8)
        qs_rest = kept("qs_rest", [P, 2, N - W], U8)
        vs = kept("vs", [P, CHUNKS, D], U8)
        r_row = kept("r_row", [P, N], BF16)
        z_cols = kept("z_cols", [P, P], F32)
        z_parts = kept("z_parts", [P, TILES * CHUNKS], F32)
        ident = kept("ident", [P, P], F32)
        ones = kept("ones", [P, P], BF16)

        nc.gpsimd.memset(z_cols[:], 0.0)
        nc.gpsimd.memset(qs_first[:].rearrange("p g n -> p (g n)").bitcast(I32), 0)
        nc.vector.memset(r_row[:].bitcast(I32), 0)
        nc.vector.memset(qs_rest[:].rearrange("p g n -> p (g n)").bitcast(I32), 0)
        nc.vector.memset(vs[:].rearrange("p g n -> p (g n)").bitcast(I32), 0)
        make_identity(nc, ident[:])
        nc.scalar.activation(out=ones[:], in_=z_cols[:], func=ACT.Exp)

        warm = bank("warm", [P, P])
        for w in range(WARM_UPS):
            nc.tensor.matmul(warm[:], lhsT=z_cols[:], rhs=z_cols[:], start=True, stop=True)

        rows = {}
        b_raw, qv = {}, {}
        v = kept("v", [P, CHUNKS, 2 * D], U8)

        def load_x(i):
            rows["x%d" % i] = kept("x%d" % i, [P, D], BF16)
            nc.sync.dma_start(out=rows["x%d" % i][:], in_=x[i * P : (i + 1) * P, :])

        def load_y(a):
            rows["y%d" % a] = kept("y%d" % a, [P, 2 * R], BF16)
            nc.sync.dma_start(
                out=rows["y%d" % a][:].rearrange("p (a k) -> p a k", a=2),
                in_=y[2 * a * P : 2 * (a + 1) * P, :].rearrange("(a p) k -> p a k", a=2),
            )

        def load_b(j):
            b_raw[j] = kept("b_raw%d" % j, [P, 4, W], BF16)
            nc.sync.dma_start(out=b_raw[j][:], in_=b[:, j * W : (j + 1) * W].rearrange("(p t) n -> p t n", t=4))

        def load_qv(j, count):
            both = kept("qv%d" % j, [P, 2, count * 2 * W], U8)
            for c in range(count):
                qv[j + c] = both[:, :, c * 2 * W : (c + 1) * 2 * W]
            nc.sync.dma_start(
                out=both[:].bitcast(I32),
                in_=qv_words.bitcast(I32)[:, :, j * W // 2 : (j + count) * W // 2].rearrange("g p n -> p g n"),
            )

        def load_scales(plane, scales, c0, c1):
            by_row = scales.bitcast(I32)[:, :, c0 // 4 : c1 // 4].rearrange("g (q s) n -> s q g n", s=4)
            for s in range(4):
                nc.sync.dma_start(out=plane[s:P:32].bitcast(I32), in_=by_row[s])

        load_x(0)
        load_y(0)
        load_scales(qs_first, qv_scales, 0, W)
        nc.sync.dma_start(out=r_row[0:1, :], in_=r.rearrange("(o n) -> o n", o=1))
        load_b(0)
        load_qv(0, 1)
        load_x(1)
        load_x(2)
        load_y(1)
        load_x(3)
        load_b(1)
        load_qv(1, 1)
        load_scales(qs_rest, qv_scales, W, N)
        load_b(2)
        load_qv(2, 2)
        load_b(3)
        load_y(2)
        load_x(4)
        load_x(5)
        load_scales(vs, v_scales, 0, D)
        nc.sync.dma_start(out=v[:].bitcast(I32), in_=v_words.bitcast(I32).rearrange("g p n -> p g n"))

        engines = {"S": nc.scalar.copy, "V": nc.vector.tensor_copy}
        in_order, grouped, codes, scales = {}, {}, {}, {}
        b_grouped, r_sorted, g_bank, e = {}, {}, {}, {}

        def presort(u):
            in_order[u] = ringed("sorted", 4, "sorted_" + u, [P, 4, P], F32)
            nc.vector.tensor_copy(
                out=in_order[u][:].rearrange("p (g u) (c i) -> p g c u i", u=2, i=4),
                in_=rows[u][:, :].bitcast(F32).rearrange("p (g c i u) -> p g c u i", g=2, i=4, u=2),
            )

        def turn(units, engs):
            banks = []
            for u in units:
                t = bank("t_" + u, [P, 4, P])
                banks.append(t)
                for q in range(4):
                    if u in in_order:
                        src = in_order[u][:, q, :]
                    else:
                        src = rows[u][:, :].bitcast(F32)[:, 256 * (q // 2) + q % 2 : 256 * (q // 2 + 1) : 2]
                    nc.tensor.transpose(t[:, q, :], src, ident[:])
            for u, t, eng in zip(units, banks, engs):
                grouped[u] = ringed("grouped", 8, "grouped_" + u, [P, 2 * W], BF16)
                engines[eng](
                    out=grouped[u][:].bitcast(F32).rearrange("p (a m u) -> p a m u", a=2, u=2),
                    in_=t[:].rearrange("p (a u) m -> p a m u", u=2),
                )

        def quantise(key, src, width):
            codes[key] = kept("codes_" + key, [P, width], U32)
            scales[key] = kept("scales_" + key, [P, width], U8)
            nc.vector.quantize_mx(out=codes[key][:].bitcast(FP8X4), scales=scales[key][:], in_=src)

        def quant(units):
            for u in units:
                quantise(u, grouped[u][:], 2 * P)

        def interleave(j, eng, c0, c1):
            if j not in b_grouped:
                b_grouped[j] = ringed("b_grouped", 2, "b_grouped%d" % j, [P, W, 4], BF16)
            engines[eng](
                out=b_grouped[j][:, c0:c1, :].rearrange("p (c i) t -> p c t i", i=4),
                in_=b_raw[j][:, :, c0:c1].rearrange("p t (c i) -> p c t i", i=4),
            )

        def quant_b(j):
            quantise("b%d" % j, b_grouped[j][:].rearrange("p n t -> p (n t)"), W)

        r_bank = {}

        def spread_r(j):
            r_bank[j] = bank("r_bank%d" % j, [P, W])
            nc.tensor.matmul(r_bank[j][:], lhsT=ones[:], rhs=r_row[:, j * W : (j + 1) * W], start=True, stop=True)

        def fetch_r(j, eng):
            r_sorted[j] = kept("r_sorted%d" % j, [P, W], BF16)
            engines[eng](
                out=r_sorted[j][:].rearrange("m (u p e) -> m u p e", u=2, e=2),
                in_=r_bank[j][:].rearrange("m (p u e) -> m u p e", u=2, e=2),
            )

        def mx(acc, key, half, rhs, rhs_scale, start, stop):
            cols = slice(half * P, (half + 1) * P)
            nc.tensor.matmul_mx(
                out=acc[:], lhsT=codes[key][:, cols].bitcast(FP8X4), lhsT_scale=scales[key][:, cols],
                rhs=rhs, rhs_scale=rhs_scale, start=start, stop=stop,
            )

        def grad_x(s):
            i, j = order[s]
            g_bank[s] = bank("g%d" % s, [P, W])
            for g in range(2):
                plane = qs_first[:, g, :] if j == 0 else qs_rest[:, g, (j - 1) * W : j * W]
                mx(g_bank[s], "x%d" % i, g, qv[j][:, g, :].bitcast(FP4X4), plane, g == 0, False)

        def grad_y(s):
            i, j = order[s]
            key = "b%d" % j
            mx(g_bank[s], "y%d" % (i // 2), i % 2, codes[key][:].bitcast(FP8X4), scales[key][:], False, True)
            e[s] = ringed("e", 14, "e%d" % s, [P, W], F32)
            col = i * CHUNKS + j
            nc.scalar.activation(
                out=e[s][:].rearrange("m (u p e) -> m u p e", u=2, e=2),
                in_=g_bank[s][:].rearrange("m (p u e) -> m u p e", u=2, e=2),
                func=ACT.Exp, scale=-1.0, accum_out=z_parts[:, col : col + 1],
            )

        h_rows = {}

        def weigh(s):
            u = "h%d" % (s // 2)
            if s % 2 == 0:
                h_rows[u] = ringed("h_rows", 9, "rows_" + u, [P, 2 * W], BF16)
                in_order[u] = h_rows[u][:, :].bitcast(F32).rearrange("p (q w) -> p q w", q=4)
            half = s % 2
            nc.vector.tensor_tensor(
                out=h_rows[u][:, half * W : (half + 1) * W], in0=e[s][:], in1=r_sorted[order[s][1]][:], op=ALU.mult
            )

        def step_cols(i, c0, width, eng):
            acc = bank("o%d_%d" % (i, c0), [P, width])
            for j in range(CHUNKS):
                s = order.index((i, j))
                words = v[:, j, 2 * c0 : 2 * (c0 + width)]
                mx(acc, "h%d" % (s // 2), s % 2, words.bitcast(FP4X4), vs[:, j, c0 : c0 + width], j == 0, j == CHUNKS - 1)
            res = ringed("res", 6, "res%d_%d" % (i, c0), [P, width], F32)
            engines[eng](out=res[:], in_=acc[:])
            nc.sync.dma_start(out=out_0[i * P : (i + 1) * P, c0 : c0 + width], in_=res[:])

        turn(["x0", "y0"], "SV")
        for j in range(CHUNKS):
            spread_r(j)
        quant(["x0"])
        fetch_r(0, "S")
        interleave(0, "V", 0, B0_VECTOR_COLS)
        interleave(0, "S", B0_VECTOR_COLS, W)
        quant(["y0"])
        fetch_r(1, "V")
        quant_b(0)
        grad_x(0)
        fetch_r(2, "V")
        fetch_r(3, "S")
        turn(["x1", "x2", "y1", "x3"], "SSSS")
        quant(["x1"])
        grad_y(0)
        quant(["x2", "y1", "x3"])
        interleave(1, "V", 0, B1_VECTOR_COLS)
        interleave(1, "S", B1_VECTOR_COLS, W)
        quant_b(1)

        late_rows = ["y2", "x4", "x5"]
        first_h = ["h0", "h2", "h4", "h6"]
        second_h = ["h1", "h3", "h5", "h7"]
        third_h = ["h8", "h9", "h10", "h11"]
        to_weigh = [s for s in range(16) if s % 4 < 2] + [s for s in range(16) if s % 4 >= 2] + list(range(16, 24))
        for s in range(1, len(order)):
            if s == 13:
                turn(late_rows, "SSS")
            if s == 19:
                turn(first_h, "SSSS")
            if s in (4, 7):
                interleave(2 + (s - 4) // 3, "V", 0, W)
            if s in (5, 8):
                quant_b(2 + (s - 5) // 3)
            if s == 10:
                for u in late_rows:
                    presort(u)
            if s in (4, 8):
                grad_x(s)
                grad_x(s + 1)
            elif s not in (5, 9):
                grad_x(s)
            grad_y(s)
            if s == 13:
                quant(late_rows)
            if s == 20:
                quant(first_h)
            if s >= 11 and s != 13:
                for t in [t for t in to_weigh if t < s][:2]:
                    weigh(t)
                    to_weigh.remove(t)
        weigh(len(order) - 1)
        nc.vector.tensor_reduce(
            out=z_cols[:, 0:TILES], in_=z_parts[:].rearrange("p (i j) -> p i j", j=CHUNKS), axis=mybir.AxisListType.X, op=ALU.add
        )
        turn(second_h, "SSSS")
        step_cols(0, 0, W, "S")
        quant(second_h)
        step_cols(0, W, W, "S")
        step_cols(1, 0, W, "V")
        step_cols(1, W, W, "S")
        turn(third_h, "VSVS")
        z_bank = bank("z_bank", [P, P])
        nc.tensor.transpose(z_bank[:], z_cols[:], ident[:])
        quant(third_h)
        z_rows = kept("z_rows", [32, P], F32)
        nc.scalar.activation(out=z_rows[:], in_=z_bank[0:32, :], func=ACT.Copy, scale=1.0 / N)
        nc.sync.dma_start(out=out_1.rearrange("(i p) -> i p", p=P), in_=z_rows[0:TILES, :])
        for i in (2, 3, 4):
            step_cols(i, 0, W, "V")
            step_cols(i, W, W, "S")
        step_cols(5, 0, W, "V")
        for c in range(4):
            step_cols(5, W + c * P, P, "SV"[c % 2])
